import numpy as np, ml_dtypes
CORES = [8,80,112,136,208,240,264,336,368,392,464,496]
N = 12
import mx_ref
NC, G, D = 128, 2, 4
C = np.float32(0.047)
BF = ml_dtypes.bfloat16
def cut(t, i, w=512):
    return t[:, w * i:w * i + w]
def tile(rs):
    return np.stack(rs, axis=2).reshape(128, -1).astype(BF)
def layer(w, X):
    out = []
    for i in range(G):
        for t in range(len(X)):
            p = mx_ref.matmul(mx_ref.quantize(cut(w, len(X) * i + t)), X[t])
            z = p if t == 0 else z + p
        out.append(z)
    return out
def act(Z):
    return [np.maximum(s * z, 0) * C for z in Z for s in (1, -1)]
def setup_inputs(rng):
    def f(*shape):
        return mx_ref.flush((rng.standard_normal(shape, dtype=np.float32) * np.exp2(rng.integers(-2, 3, shape[:-1] + (1,)))).astype(BF))
    return {"x": f(N, 128, 4 * NC), "w1": np.broadcast_to(f(1, 128, G * 512), (N, 128, G * 512)).copy(), "wt": f(N, 128, 3 * 512)}
def setup_inputs_blocks(rng):
    d = setup_inputs(rng)
    for k in ("x", "wt"): d[k] = mx_ref.spread(d[k], rng, 2)
    return d
def setup_inputs_wide(rng):
    d = setup_inputs(rng)
    for k in ("wt",): d[k] = mx_ref.flush((d[k].astype(np.float32) * np.exp2(rng.integers(-6, 7, (N, 1, 1))).astype(np.float32)).astype(BF))
    return d
def setup_inputs_zeros(rng):
    d = setup_inputs(rng); v = d["x"].reshape(N, 128, -1, 4).copy()
    v[np.broadcast_to((rng.random((N, 1, v.shape[2], 1)) < 0.33), v.shape)] = 0
    d["x"] = v.reshape(d["x"].shape)
    return d
def reference(x, w1, wt):
    h = [tile(act(layer(w1[j], [mx_ref.quantize(x[j])]))) for j in range(N)]
    y = np.zeros((N, 128, NC), np.float32)
    for r in range(N):
        e = np.concatenate([h[(r - 1) % N][:, 4 * (NC - D):], h[r], h[(r + 1) % N][:, :4 * D]], axis=1)
        for t in range(3):
            p = mx_ref.matmul(mx_ref.quantize(cut(wt[r], t)), mx_ref.quantize(e[:, 4 * D * t:4 * D * t + 4 * NC]))
            y[r] = p if t == 0 else y[r] + p
    return {"y": y}

from concourse.bass import DstId, RemoteDMATransfer
from concourse.mybir import dt, AluOpType, ActivationFunctionType

WORLD = 512
NC, D = 128, 4
C = 0.047
K_RANK = 4
K_FAR = 8

F8, BF, U8, F32 = "float8_e4m3fn_x4", "bfloat16", "uint8", "float32"
SCRATCH = {
    "xt": ("sbuf", [128, 512], BF),
    "w1t": ("sbuf", [128, 1024], BF),
    "wtt": ("sbuf", [128, 1536], BF),
    "ht": ("sbuf", [128, 512], BF),
    "qx": ("sbuf", [128, 144], F8), "sx": ("sbuf", [128, 144], U8),
    "qw": ("sbuf", [128, 256], F8), "sw": ("sbuf", [128, 256], U8),
    "qt": ("sbuf", [128, 384], F8), "st": ("sbuf", [128, 384], U8),
    "qh": ("sbuf", [128, 256], F8), "sh": ("sbuf", [128, 256], U8),
    "qg": ("sbuf", [128, 128], F8), "sg": ("sbuf", [128, 128], U8),
    "rc": ("sbuf", [128, 8], F8), "rs": ("sbuf", [128, 32], U8),
    "ys": ("sbuf", [128, 128], F32),
    "ps": ("psum", [128, 512 * 7], F32),
}
SEMAPHORES = ["x_in", "w1_in", "wt_in", "x_q", "w1_q", "wt_q", "z0", "z1", "h_made", "h_q", "mid",
              "arr", "zh0", "zh1", "g_made", "g_q", "left", "right", "y_made", "y_out", "go", "sent", "land"]


def engines(avail, first, k):
    on = [e for e in range(16) if avail >> e & 1]
    return sum(1 << e for e in on[first:first + k])


def neighbours(T, r):
    n = len(T.cores)
    return [T.cores[(r - 1) % n], T.cores[(r + 1) % n]]


def split(T, topo, r):
    ok = [topo.may_write(T.cores[r], d) for d in neighbours(T, r)]
    return [e for e in (0, 1) if not ok[e]], [e for e in (0, 1) if ok[e]]


def same_chip(topo, a, b):
    return topo.host(a) == topo.host(b) and topo.chip(a) == topo.chip(b)


def relays(T, topo, r):
    me, far = T.cores[r], [neighbours(T, r)[e] for e in split(T, topo, r)[0]]
    if not far:
        return []
    return [c for c in range(WORLD) if same_chip(topo, c, me) and c != me and topo.die(c) == topo.die(me)
            and all(topo.may_write(c, d) for d in far)][:2]


def stand(e):
    return NC // 2 - D * e


def place(e):
    return NC + D * (1 - e)


def arrivals(T, topo, r):
    n, total = len(T.cores), 0
    for e, s in ((1, (r - 1) % n), (0, (r + 1) % n)):
        far, near = split(T, topo, s)
        total += 2 * (K_FAR if e in near else K_FAR // len(far))
    return total


def codes(ap):
    return ap.bitcast(dt.uint8)


def rank_program(g, core, T, topo):
    rank = T.rank_of(core)
    if rank is not None:
        send_edges(g, core, T, topo, rank)
        compute(g, core, T, topo, rank)
        return
    for r, me in enumerate(T.cores):
        if same_chip(topo, core, me):
            team = relays(T, topo, r)
            if core in team:
                relay(g, core, T, topo, r, team.index(core))


def relay(g, core, T, topo, r, scales):
    s, far, to = T.sem, split(T, topo, r)[0], neighbours(T, r)
    k, lo = K_FAR // len(far), min(stand(e) for e in far)
    moves = []
    for i, e in enumerate(far):
        rid, pid = topo.addr(to[e], core)
        a, b = stand(e) - lo, place(e)
        if scales:
            src, dst = T.rs[:, a:a + D], T.sx[:, b:b + D]
        else:
            src, dst = codes(T.rc[:, a:a + D]), codes(T.qx[:, b:b + D])
        moves.append((src, dst, rid, pid, engines(topo.mask(core, to[e]), k * i, k)))
    g.wait_ge(s.land, K_RANK)
    if len(moves) == 1:
        src, dst, rid, pid, m = moves[0]
        g.remote_dma(out_ap=dst, in_ap=src, remote_sem=s.arr, local_sem=s.sent, pid=pid, routing_id=rid, dma_engine_mask=m)
    else:
        g.remote_dma_fused([RemoteDMATransfer(dst_ids=[DstId(rid=rid, pnc=pid)], dma_engine_mask=m, remote_sem=s.arr,
                                              src=src, dst=dst) for src, dst, rid, pid, m in moves], local_sem=s.sent)
    g.wait_ge(s.sent, k * len(far))


def send_edges(g, core, T, topo, r):
    s, to = T.sem, neighbours(T, r)
    far, near = split(T, topo, r)
    total = 0
    g.wait_ge(s.x_q, 1)
    if far:
        lo, n = min(stand(e) for e in far), D * len(far)
        moves = []
        for i, c in enumerate(relays(T, topo, r)):
            rid, pid = topo.addr(c, core)
            src, dst = ((T.sx[:, lo:lo + 4 * n], T.rs[:, 0:4 * n]) if i else
                        (codes(T.qx[:, lo:lo + n]), codes(T.rc[:, 0:n])))
            moves.append(RemoteDMATransfer(dst_ids=[DstId(rid=rid, pnc=pid)], remote_sem=s.land, src=src, dst=dst,
                                           dma_engine_mask=engines(topo.mask(core, c), K_RANK * i, K_RANK)))
        g.remote_dma_fused(moves, local_sem=s.sent)
        total += 2 * K_RANK
    g.sem_inc(s.go, 1)
    for e in near:
        rid, pid = topo.addr(to[e], core)
        a, b = stand(e), place(e)
        for src, dst in ((codes(T.qx[:, a:a + D]), codes(T.qx[:, b:b + D])), (T.sx[:, a:a + D], T.sx[:, b:b + D])):
            g.remote_dma(out_ap=dst, in_ap=src, remote_sem=s.arr, local_sem=s.sent, pid=pid, routing_id=rid,
                         dma_engine_mask=engines(topo.mask(core, to[e]), 0, K_FAR))
            total += K_FAR
    g.wait_ge(s.sent, total)


def compute(g, core, T, topo, r):
    s, te, ve, sc, sy = T.sem, g.tensor, g.vector, g.scalar, g.sync
    X, H, W = 4 * NC, T.ht, 512

    def bank(i, a=0, b=NC):
        return T.ps[:, W * i + a:W * i + b]

    Z0, Z1, G0, G1, MID, LEFT, RIGHT = range(7)

    sy.dma_start(T.xt[:, 0:X // 2], T.x[:, X // 2:X]).then_inc(s.x_in, 16)
    sc.dma_start(T.xt[:, X // 2:X], T.x[:, 0:X // 2]).then_inc(s.x_in, 16)
    sc.dma_start(T.w1t[:], T.w1[:]).then_inc(s.w1_in, 16)
    sy.wait_ge(s.go, 1)
    sy.dma_start(T.wtt[:], T.wt[:]).then_inc(s.wt_in, 16)

    ve.wait_ge(s.x_in, 32)
    ve.quantize_mx(T.qx[:, 0:NC], T.sx[:, 0:NC], T.xt[:]).then_inc(s.x_q, 1)
    ve.wait_ge(s.w1_in, 16)
    for i in range(2):
        a = NC * i
        ve.quantize_mx(T.qw[:, a:a + NC], T.sw[:, a:a + NC], T.w1t[:, W * i:W * i + W]).then_inc(s.w1_q, 1)

    def by_w1(i, b, a):
        w = NC * i
        return te.matmul_mx(bank(b), T.qw[:, w:w + NC], T.sw[:, w:w + NC], T.qx[:, a:a + NC], T.sx[:, a:a + NC], True, True)

    te.wait_ge(s.x_q, 1)
    te.wait_ge(s.w1_q, 2)
    by_w1(0, Z0, 0).then_inc(s.z0, 1)
    by_w1(1, Z1, 0).then_inc(s.z1, 1)

    for i, (z, b) in enumerate(((s.z0, Z0), (s.z1, Z1))):
        sc.wait_ge(z, 1)
        for j, c in enumerate((C, -C)):
            sc.activation(H[:, 2 * i + j:X:4], bank(b), ActivationFunctionType.Relu, scale=c).then_inc(s.h_made, 1)
    ve.wait_ge(s.h_made, 4)
    for a in (0, NC):
        ve.quantize_mx(T.qh[:, a:a + NC], T.sh[:, a:a + NC], H[:]).then_inc(s.h_q, 1)
    ve.wait_ge(s.wt_in, 16)
    for t in range(3):
        a = NC * t
        ve.quantize_mx(T.qt[:, a:a + NC], T.st[:, a:a + NC], T.wtt[:, W * t:W * t + W]).then_inc(s.wt_q, 1)

    def tap(t, b, q, sq, a, start, stop):
        w = NC * t
        return te.matmul_mx(bank(b), T.qt[:, w:w + NC], T.st[:, w:w + NC], q[:, a:a + NC], sq[:, a:a + NC], start, stop)

    def own(t, b, token, start, stop):
        return tap(t, b, T.qh, T.sh, (token + NC // 2) % NC, start, stop)

    te.wait_ge(s.h_q, 2)
    te.wait_ge(s.wt_q, 3)
    own(0, MID, -D, True, False)
    own(1, MID, 0, False, False)
    own(2, MID, D, False, True).then_inc(s.mid, 1)
    own(1, LEFT, 0, True, False)
    own(2, LEFT, D, False, False)
    own(0, RIGHT, NC - 3 * D, True, False)
    own(1, RIGHT, NC - 2 * D, False, False)
    ve.wait_ge(s.mid, 1)
    ve.tensor_copy(T.ys[:, D:NC - D], bank(MID, D, NC - D)).then_inc(s.y_made, 1)

    te.wait_ge(s.arr, arrivals(T, topo, r))
    by_w1(0, G0, 2 * D).then_inc(s.zh0, 1)
    by_w1(1, G1, 2 * D).then_inc(s.zh1, 1)
    ve.wait_ge(s.h_q, 2)
    for i, (z, b) in enumerate(((s.zh0, G0), (s.zh1, G1))):
        ve.wait_ge(z, 1)
        for j, c in enumerate((C, -C)):
            ve.tensor_scalar(H[:, 2 * i + j:8 * D:4], bank(b, NC - 2 * D, NC), c, 0.0, AluOpType.mult,
                             AluOpType.max).then_inc(s.g_made, 1)
    ve.wait_ge(s.g_made, 4)
    ve.quantize_mx(T.qg[:], T.sg[:], H[:]).then_inc(s.g_q, 1)
    te.wait_ge(s.g_q, 1)
    tap(0, LEFT, T.qg, T.sg, 0, False, True).then_inc(s.left, 1)
    tap(2, RIGHT, T.qg, T.sg, 0, False, True).then_inc(s.right, 1)
    ve.wait_ge(s.left, 1)
    ve.tensor_copy(T.ys[:, 0:D], bank(LEFT, 0, D)).then_inc(s.y_made, 1)
    ve.wait_ge(s.right, 1)
    ve.tensor_copy(T.ys[:, NC - D:NC], bank(RIGHT, D, 2 * D)).then_inc(s.y_made, 1)
    sy.wait_ge(s.y_made, 3)
    sy.dma_start(T.y[:], T.ys[:]).then_inc(s.y_out, 16)
    sy.wait_ge(s.y_out, 16)
